import numpy as np, ml_dtypes
CORES = [10,34,74,98]
N = 4
BF = ml_dtypes.bfloat16
def gentries(a):
    return np.ascontiguousarray(a.reshape(8, 16, -1).transpose(0, 2, 1)).reshape(8, -1)
def gtable(e):
    e = np.asarray(e); return np.ascontiguousarray(e.reshape(8, -1, 16).transpose(0, 2, 1)).reshape(128, -1).astype(np.int32)
P, A, M, Q = 16384, 16, 8, 512
S = N * P
def letters(rng, w, n):
    a = np.add.accumulate(w); return np.searchsorted(a[:-1], rng.random(n) * a[-1], side="right")
def places(rng):
    p = rng.integers(0, S + 1, (N, 8, 2, Q)); u = P // 8
    v = rng.integers(0, 8 * N + 1, p.shape) * u + rng.integers(-1, 2, p.shape)
    p = np.sort(np.where(rng.random(p.shape) < 0.25, np.minimum(np.maximum(v, 0), S), p), axis=2)
    k = (8 * np.arange(N)[:, None] + np.arange(8)) * u
    p[:, :, 0, Q - 5] = k; p[:, :, 1, Q - 5] = k + u; p[:, :, :, Q - 4] = S; p[:, :, :, Q - 3] = 0
    p[:, :, 1, Q - 2] = p[:, :, 0, Q - 2]; p[:, :, 0, Q - 1] = 0; p[:, :, 1, Q - 1] = S
    return p
def pack(s, e, p):
    return {"bwt": np.ascontiguousarray(np.asarray(s).reshape(8, N, P).transpose(1, 0, 2)).astype(np.int32), "pats": np.stack([gtable(e[r].reshape(8, M * Q)) for r in range(N)]), "starts": np.stack([gtable(p[r].reshape(8, 2 * Q)) for r in range(N)])}
def bw(t):
    n = len(t); key = np.zeros(n, np.int64); k = 62 // (A - 1).bit_length()
    for i in range(k): key = key * A + np.roll(t, -i)
    while True:
        o = np.argsort(key); ks = key[o]
        v = np.zeros(n, np.int64); v[o[1:]] = np.add.accumulate((ks[1:] != ks[:-1]).astype(np.int64))
        if v.max() == n - 1 or k >= n: break
        key = (v * n + np.roll(v, -k)) * n + np.roll(v, -2 * k); k *= 3
    return t[o - 1]
def setup_inputs(rng):
    s = []; e = rng.integers(0, A, (N, 8, M, Q)); h = Q // 2
    for g in range(8):
        w = np.exp2(rng.integers(0, 4, A)); c = rng.integers(0, A); w[c] += 4 * A
        s.append(np.concatenate([letters(rng, w * np.exp2(rng.integers(0, 3, A)), P) for r in range(N)]))
        e[:, g, :, :h] = np.where(rng.random((N, M, h)) < 0.875, c, e[:, g, :, :h])
    return pack(np.stack(s), e, places(rng))
def setup_inputs_ends(rng):
    i = np.arange(S); s = np.zeros((8, S), np.int64)
    s[0] = i * A // S; s[1] = A - 1 - s[0]; s[2] = i % A; s[3] = rng.integers(0, A - 1, S); s[4] = rng.integers(1, A, S); s[5] = i // P % A
    s[6] = np.where((i % P == 0) | (i % P == P - 1), A - 1, rng.integers(0, A - 1, S)); s[7] = np.where(i == S - 1, A - 1, rng.integers(0, A - 1, S))
    e = rng.integers(0, A, (N, 8, M, Q)); e[..., 0] = 0; e[..., 1] = A - 1; e[..., 2] = 0; e[:, :, 0, 2] = A - 1; e[..., 3] = 0; e[:, :, M - 1, 3] = A - 1
    q = rng.integers(0, N); e[q] = rng.integers(0, A, (8, M, 1)); e[q, 0] = e[q, 0, 0, 0]
    p = places(rng); p[:, :, 0, :4] = 0; p[:, :, 1, :4] = S; p[q, :, 0] = 0; p[q, :, 1] = S
    return pack(s, e, p)
def setup_inputs_one(rng):
    k = (np.arange(8) + rng.integers(0, A)) % A; c = k[None, :, None, None]
    e = np.where(rng.random((N, 8, 1, Q)) < 0.5, c, rng.integers(0, A, (N, 8, M, Q))); e[..., 0] = k[None, :, None]
    return pack(np.repeat(k[:, None], S, axis=1), e, places(rng))
def setup_inputs_text(rng):
    s = []; e = np.zeros((N, 8, M, Q), np.int64); h = Q // 2
    for g in range(8):
        t = np.tile(letters(rng, np.exp2(rng.integers(0, 3, A)), S // 8), 8); t = np.where(rng.random(S) < 0.03125, rng.integers(0, A, S), t); s.append(bw(t))
        e[:, g] = t[(rng.integers(0, S, (N, 1, Q)) + (M - 1 - np.arange(M))[None, :, None]) % S]
    e[..., h:] = np.where(rng.random((N, 8, M, Q - h)) < 0.0625, rng.integers(0, A, (N, 8, M, Q - h)), e[..., h:])
    p = places(rng); p[:, :, 0, :h] = 0; p[:, :, 1, :h] = S
    return pack(np.stack(s), e, p)
def setup_inputs_spread(rng):
    s = np.stack([np.concatenate([letters(rng, np.exp2(-2.0 * rng.permutation(A)), P) for r in range(N)]) for g in range(8)])
    e = np.stack([s[g][rng.integers(0, S, (N, M, Q))] for g in range(8)], axis=1)
    p = places(rng); p[:, :, 1] = np.minimum(p[:, :, 0] + (rng.integers(0, S + 1, (N, 8, Q)) >> rng.integers(0, 20, (N, 8, Q))), S)
    return pack(s, np.where(rng.random((N, 8, 1, Q)) < 0.5, e, rng.integers(0, A, (N, 8, M, Q))), p)
def check_inputs(d):
    bad = [k + " out of range" for k in ("bwt", "pats") if not ((d[k] >= 0) & (d[k] < A)).all()]
    if not ((d["starts"] >= 0) & (d["starts"] <= S)).all(): bad.append("starts out of range")
    p = np.stack([gentries(a) for a in d["starts"]]).reshape(N, 8, 2, Q)
    if (p[:, :, 0] > p[:, :, 1]).any(): bad.append("lo over hi in starts")
    return bad
def reference(bwt, pats, starts):
    s = bwt.transpose(1, 0, 2).reshape(8, S)
    e = np.stack([gentries(pats[r]) for r in range(N)]).reshape(N, 8, M, Q)
    b = np.stack([gentries(starts[r]) for r in range(N)]).reshape(N, 8, 2, Q).astype(np.int64)
    ends = np.zeros((N, 8, 2, Q), np.int64)
    for g in range(8):
        C = np.array([np.count_nonzero(s[g] < c) for c in range(A)]); occ = np.zeros((A, S + 1), np.int64)
        for c in range(A): occ[c, 1:] = np.add.accumulate((s[g] == c).astype(np.int64))
        p = b[:, g]
        for t in range(M):
            c = e[:, g, t][:, None]; p = C[c] + occ[c, p]
        ends[:, g] = p
    return {"y": np.asarray(np.stack([gtable(ends[r].reshape(8, 2 * Q)) for r in range(N)]), np.float32)}

@@ -1,0 +1,302 @@
+from concourse.bass import DstId, RemoteDMATransfer
+from concourse.mybir import AluOpType as Op, ActivationFunctionType as Fn
+
+R, B = 4, 1024
+NB = R * B
+STR = 4224
+W = 2 * STR
+ASW = 1032
+
+SCRATCH = {
+    "raw": ("sbuf", [128, 64, 16], "int32"),
+    "half": ("sbuf", [128, 8, 128], "bfloat16"),
+    "let": ("sbuf", [128, B], "bfloat16"),
+    "keyw": ("sbuf", [128, W], "bfloat16"),
+    "base": ("sbuf", [128, W], "bfloat16"),
+    "feat": ("sbuf", [128, 16 * B], "bfloat16"),
+    "sums": ("sbuf", [128, 2 * ASW], "bfloat16"),
+    "hd": ("sbuf", [128, 2 * B], "bfloat16"),
+    "tot": ("sbuf", [128, R, 8], "float32"),
+    "t2": ("sbuf", [128, R, 2], "float32"),
+    "pre": ("sbuf", [128, R, 2], "float32"),
+    "rr": ("sbuf", [128, 8], "float32"),
+    "q1": ("sbuf", [128, 2], "float32"),
+    "init": ("sbuf", [128, 2], "float32"),
+    "wv": ("sbuf", [128, 2], "float32"),
+    "wd": ("sbuf", [128, 2], "bfloat16"),
+    "gi": ("sbuf", [128, 128], "bfloat16"),
+    "j1": ("sbuf", [128, 128], "bfloat16"),
+    "j8": ("sbuf", [128, 128], "bfloat16"),
+    "d0": ("sbuf", [128, 128], "bfloat16"),
+    "lp": ("sbuf", [128, 1], "int32"),
+    "li": ("sbuf", [128, 4], "int32"),
+    "lf": ("sbuf", [128, 4], "float32"),
+    "ma": ("sbuf", [128, 128], "bfloat16"),
+    "mb": ("sbuf", [128, 128], "bfloat16"),
+    "bm": ("sbuf", [128, 128], "bfloat16"),
+    "f16": ("sbuf", [128, 128], "bfloat16"),
+    "f8": ("sbuf", [128, 128], "bfloat16"),
+    "lfm": ("sbuf", [128, 8 * 128], "bfloat16"),
+    "xq": ("sbuf", [128, 16 * 128], "bfloat16"),
+    "eq": ("sbuf", [128, 16 * 128], "bfloat16"),
+    "idm": ("sbuf", [128, 128], "bfloat16"),
+    "neg": ("sbuf", [128, 128], "bfloat16"),
+    "s1": ("sbuf", [128, 128], "float32"),
+    "s2": ("sbuf", [128, 128], "float32"),
+    "s3": ("sbuf", [128, 128], "float32"),
+    "s4": ("sbuf", [128, 128], "float32"),
+    "smf": ("sbuf", [128, 128], "float32"),
+    "swf": ("sbuf", [128, 128], "float32"),
+    "smb": ("sbuf", [128, 128], "bfloat16"),
+    "swb": ("sbuf", [128, 128], "bfloat16"),
+    "nh": ("sbuf", [128, 512], "bfloat16"),
+    "c8": ("sbuf", [128, 64], "bfloat16"),
+    "pat": ("sbuf", [128, 8, 32], "int32"),
+    "pi": ("sbuf", [128, 8, 32], "int32"),
+    "chi": ("sbuf", [128, 8, 32], "int32"),
+    "cl": ("sbuf", [128, 8, 32], "bfloat16"),
+    "ch2": ("sbuf", [128, 8, 64], "bfloat16"),
+    "c16": ("sbuf", [128, 8, 64], "bfloat16"),
+    "msk": ("sbuf", [128, 8 * 512], "bfloat16"),
+    "sti": ("sbuf", [128, 64], "int32"),
+    "xi": ("sbuf", [128, 64], "int32"),
+    "ri": ("sbuf", [128, 64], "int32"),
+    "kl": ("sbuf", [128, 2, 64], "bfloat16"),
+    "of0": ("sbuf", [128, 64], "uint16"),
+    "of1": ("sbuf", [128, 64], "uint16"),
+    "kg": ("sbuf", [128, 1024], "bfloat16"),
+    "ym": ("sbuf", [128, 1024], "bfloat16"),
+    "xs": ("sbuf", [128, 1024], "bfloat16"),
+    "yo": ("sbuf", [128, 64], "float32"),
+    "pa": ("psum", [128, 2048], "float32"),
+    "pb": ("psum", [128, 2048], "float32"),
+}
+SEMAPHORES = ["cV", "cS", "cP", "cG", "lpat", "lst", "dup", "out", "kin", "tin", "bin0", "bin1", "snt"] + ["ld%d" % k for k in range(8)]
+
+
+def rank_program(g, core, T, topo):
+    rank = T.rank_of(core)
+    if rank is None:
+        return
+    queues = {"V": g.vector, "S": g.scalar, "P": g.tensor, "G": g, "Y": g.sync}
+    total, seen = {}, {}
+
+    def need(q, deps):
+        for sem, val in deps:
+            if seen.get((q, sem), 0) < val:
+                queues[q].wait_ge(T.sem[sem], val)
+                seen[(q, sem)] = val
+
+    def run(q, deps, f, *a, **kw):
+        need(q, deps)
+        sem = "c" + q
+        f(*a, **kw).then_inc(T.sem[sem], 1)
+        total[sem] = total.get(sem, 0) + 1
+        return (sem, total[sem])
+
+    def dma(q, deps, sem, out, in_):
+        need(q, deps)
+        queues[q].dma_start(out, in_).then_inc(T.sem[sem], 16)
+        total[sem] = total.get(sem, 0) + 16
+        return (sem, total[sem])
+
+    v, s, pe = g.vector, g.scalar, g.tensor
+    others = [c for c in T.cores if c != core]
+    mask = topo.mask(core, others[0])
+    for c in others[1:]:
+        mask &= topo.mask(core, c)
+    width = bin(mask).count("1")
+    ids = []
+    for c in others:
+        rid, pid = topo.addr(c)[:2]
+        ids.append(DstId(rid=rid, pnc=pid))
+
+    def send(deps, piece, sem):
+        need("G", deps)
+        g.remote_dma_fused([RemoteDMATransfer(dst_ids=ids, dma_engine_mask=mask, remote_sem=T.sem[sem],
+                                              srcs=[piece], dsts=[piece for _ in ids], alu_op=0)],
+                           local_sem=T.sem.snt)
+        total["snt"] = total.get("snt", 0) + width
+
+    arrived = width * len(others)
+
+    ld = []
+    for k in range(8):
+        j, y = k // 2, k % 2
+        ld.append(dma("Y" if k % 2 == 0 else "S", [], "ld%d" % k, T.raw[:, 8 * k:8 * k + 8, :],
+                      T.bwt[y::2, 4096 * j:4096 * j + 4096]))
+    lpat = dma("Y", [], "lpat", T.pat[:, :, :], T.pats[:, :])
+    lst = dma("Y", [], "lst", T.sti[:, :], T.starts[:, :])
+
+    fl = dict(allow_small_or_imprecise_dtypes=True)
+    g_lp = run("G", [], g.iota, T.lp[:, :], [[0, 1]], 0, 1)
+    g_gi = run("G", [], g.iota, T.gi[:, :], [[-16, 8], [0, 16]], 0, 1, **fl)
+    g_j8 = run("G", [], g.iota, T.j8[:, :], [[0, 16], [1, 8]], 1, 0, **fl)
+    g_j1 = run("G", [], g.iota, T.j1[:, :], [[0, 8], [1, 16]], 1, 0, **fl)
+    g_d0 = run("G", [], g.iota, T.d0[:, :], [[-1, 128]], 0, 1, **fl)
+
+    run("V", [], v.memset, T.feat[:, 0:B], 1.0)
+    run("V", [], v.memset, T.sums[:, 0:1], 0.0)
+    run("V", [], v.memset, T.sums[:, ASW:ASW + 1], 0.0)
+    run("V", [], v.memset, T.keyw[:, NB:STR], 1024.0)
+    run("V", [], v.memset, T.base[:, NB:STR], 0.0)
+    t_ones = run("V", [], v.memset, T.base[:, STR + NB:W], 0.0)
+    run("V", [g_lp], v.tensor_scalar, T.li[:, 0:1], T.lp[:, :], 15, None, Op.bitwise_and)
+    run("V", [], v.tensor_scalar, T.li[:, 1:2], T.lp[:, :], 7, None, Op.bitwise_and)
+    t = run("V", [], v.tensor_scalar, T.li[:, 2:3], T.lp[:, :], 3, 1, Op.arith_shift_right, Op.bitwise_and)
+    run("V", [g_gi], v.tensor_scalar, T.ma[:, :], T.gi[:, :], 0.0, None, Op.is_ge)
+    t2 = run("V", [], v.tensor_scalar, T.mb[:, :], T.gi[:, :], 15.0, None, Op.is_le)
+    t_lane = run("V", [t], v.tensor_copy, T.lf[:, 0:3], T.li[:, 0:3])
+    t3 = run("V", [t2], v.tensor_tensor, T.bm[:, :], T.ma[:, :], T.mb[:, :], Op.mult)
+    t4 = run("V", [t3, g_j8], v.tensor_tensor, T.f8[:, :], T.bm[:, :], T.j8[:, :], Op.mult)
+    for y in range(8):
+        t_lfm = run("V", [t4], v.tensor_scalar, T.lfm[:, 128 * y:128 * y + 128], T.f8[:, :], float(y + 1), None, Op.is_equal)
+
+    for k in range(8):
+        j, y = k // 2, k % 2
+        t = run("V", [ld[k]], v.tensor_copy, T.half[:, :, 32 * j + 16 * y:32 * j + 16 * y + 16], T.raw[:, 8 * k:8 * k + 8, :])
+    for i in range(8):
+        t_let = run("V", [t], v.transpose, T.let[:, i::8], T.half[:, i, :])
+    t_key = run("V", [t_let, t_lane], v.tensor_scalar, T.keyw[:, B * rank:B * rank + B], T.let[:, :], 16.0, T.lf[:, 0:1], Op.mult, Op.add)
+    send([t_key], T.keyw[:, B * rank:B * rank + B], "kin")
+    dma_dup = dma("Y", [t_key, ("kin", arrived)], "dup", T.keyw[:, STR:W], T.keyw[:, 0:STR])
+
+    t_f = [t_ones]
+    for c in range(1, 16):
+        t_f.append(run("V", [], v.tensor_scalar, T.feat[:, B * c:B * c + B], T.let[:, :], float(c), None, Op.is_ge))
+    t_a = {}
+    for c in range(16):
+        for h in range(2):
+            bank = 2 * (c // 8) + h
+            t_a[bank] = run("P", [t_f[c], t_lfm], pe.matmul, T.pa[:, 512 * bank:512 * bank + 512], T.lfm[:, 128 * (c % 8):128 * (c % 8) + 128],
+                            T.feat[:, B * c + 512 * h:B * c + 512 * h + 512], c % 8 == 0, c % 8 == 7)
+    t_s = {}
+    for bank in range(4):
+        at = ASW * (bank // 2) + 1 + 512 * (bank % 2)
+        t_s[bank] = run("S", [t_a[bank], t_ones], s.activation, T.sums[:, at:at + 512], T.pa[:, 512 * bank:512 * bank + 512],
+                        Fn.Copy, scale=2.0, accum_out=T.tot[:, rank, bank:bank + 1])
+    send([t_s[3]], T.tot[:, rank, 0:4], "tin")
+
+    run("V", [g_d0], v.tensor_scalar, T.s1[:, :], T.d0[:, :], 1.0, None, Op.is_equal)
+    run("V", [], v.tensor_scalar, T.s2[:, :], T.j8[:, :], 8.0, None, Op.is_lt)
+    run("V", [], v.tensor_scalar, T.s3[:, :], T.d0[:, :], -7.0, None, Op.is_equal)
+    t = run("V", [], v.tensor_scalar, T.s4[:, :], T.j8[:, :], 8.0, None, Op.is_equal)
+    run("V", [t], v.tensor_tensor, T.smf[:, :], T.s1[:, :], T.s2[:, :], Op.mult)
+    run("V", [], v.tensor_tensor, T.swf[:, :], T.s3[:, :], T.s4[:, :], Op.mult)
+    run("V", [], v.tensor_tensor, T.smb[:, :], T.s1[:, :], T.s2[:, :], Op.mult)
+    t_sh = run("V", [], v.tensor_tensor, T.swb[:, :], T.s3[:, :], T.s4[:, :], Op.mult)
+    t_b = {}
+    for bank in range(4):
+        chi, h = bank // 2, bank % 2
+        out = T.pb[:, 512 * bank:512 * bank + 512]
+        t_b[bank] = run("P", [t_s[3], t_sh], pe.matmul, out, T.smb[:, :], T.sums[:, ASW * chi + 512 * h:ASW * chi + 512 * h + 512], True, chi == 1)
+        if chi == 0:
+            t_b[bank] = run("P", [], pe.matmul, out, T.swb[:, :], T.sums[:, ASW + 512 * h:ASW + 512 * h + 512], False, True)
+
+    run("V", [lpat], v.tensor_scalar, T.pi[:, :, :], T.pat[:, :, :], 7, None, Op.bitwise_and)
+    t = run("V", [], v.tensor_scalar, T.chi[:, :, :], T.pat[:, :, :], 3, None, Op.arith_shift_right)
+    for q in range(16):
+        t_xq = run("V", [], v.tensor_scalar, T.xq[:, 128 * q:128 * q + 128], T.gi[:, :], float(q), None, Op.is_equal)
+    t_cl = run("V", [t], v.tensor_copy, T.cl[:, :, :], T.pi[:, :, :])
+    t_m = {}
+    for st in range(8):
+        bank = st % 4
+        deps = [t_cl, t_xq, t_s[3]] + ([t_m[st - 4]] if st >= 4 else [])
+        for q in range(16):
+            lo = 512 * bank + q
+            t_ex = run("P", deps, pe.matmul, T.pa[:, lo:512 * bank + 512:16], T.xq[:, 128 * q:128 * q + 128], T.cl[:, st, :], True, True)
+        if st == 0:
+            t = run("V", [g_j1], v.tensor_tensor, T.f16[:, :], T.bm[:, :], T.j1[:, :], Op.mult)
+            for q in range(16):
+                t_eq = run("V", [t], v.tensor_scalar, T.eq[:, 128 * q:128 * q + 128], T.f16[:, :], float(q + 1), 0.5, Op.is_equal, Op.mult)
+            run("V", [], v.tensor_scalar, T.idm[:, :], T.d0[:, :], 0.0, None, Op.is_equal)
+            run("V", [], v.tensor_scalar, T.neg[:, :], T.d0[:, :], 0.0, -1.0, Op.is_equal, Op.mult)
+            run("V", [], v.memset, T.nh[:, :], -0.5)
+            run("V", [], v.memset, T.c8[:, 0:32], 8.0)
+            run("V", [], v.memset, T.c8[:, 32:64], 0.0)
+            run("V", [], v.memset, T.rr[:, :], 0.0)
+            for h in range(2):
+                run("V", [], v.tensor_scalar, T.ch2[:, :, 32 * h:32 * h + 32], T.chi[:, :, :], float(STR * 16), None, Op.mult)
+                t_ch = run("V", [], v.tensor_scalar, T.c16[:, :, 32 * h:32 * h + 32], T.pat[:, :, :], 16.0, None, Op.mult)
+            t = run("V", [t_ch, lst], v.tensor_tensor, T.xi[:, :], T.sti[:, :], T.ch2[:, 0, :], Op.add)
+            t_of = run("V", [t], v.tensor_scalar, T.of0[:, :], T.xi[:, :], 0.0625, -0.46875, Op.mult, Op.add)
+            t = run("V", [], v.tensor_scalar, T.ri[:, :], T.xi[:, :], 15, None, Op.bitwise_and)
+            t_kl = run("V", [t], v.tensor_tensor, T.kl[:, 0, :], T.ri[:, :], T.c16[:, 0, :], Op.add)
+        t_m[st] = run("V", [t_ex, t_lane], v.tensor_scalar, T.msk[:, 512 * st:512 * st + 512], T.pa[:, 512 * bank:512 * bank + 512],
+                      T.lf[:, 1:2], None, Op.is_equal)
+
+    need("V", [("tin", arrived), t_s[3]])
+    t = run("V", [], v.tensor_tensor, T.t2[:, :, :], T.tot[:, :, 0:4:2], T.tot[:, :, 1:4:2], Op.add)
+    acc, t_acc, pre = T.t2[:, 0, :], t, None
+    for r in range(1, R):
+        if r == rank:
+            pre = acc
+        dst = T.rr[:, 3:5] if r == R - 1 else T.pre[:, r, :]
+        t_acc = run("V", [t_acc], v.tensor_tensor, dst, acc, T.t2[:, r, :], Op.add)
+        acc = dst
+    t = t_acc
+    if pre is not None:
+        t = run("V", [t_acc], v.tensor_copy, T.rr[:, 0:2], pre)
+    run("P", [t, t_m[7], t_sh], pe.matmul, T.pa[:, 0:5], T.smf[:, :], T.rr[:, 0:5], True, False)
+    t_pt = run("P", [], pe.matmul, T.pa[:, 0:5], T.swf[:, :], T.rr[:, 1:6], False, True)
+    t = run("V", [t], v.tensor_tensor, T.q1[:, :], T.rr[:, 0:2], T.rr[:, 3:5], Op.subtract)
+    t = run("V", [t], v.tensor_scalar, T.q1[:, :], T.q1[:, :], float(2 * (16 * NB - 16)), None, Op.add)
+    t_in = run("V", [t, t_pt], v.tensor_tensor, T.init[:, :], T.q1[:, :], T.pa[:, 0:2], Op.subtract)
+    t_w = run("V", [], v.tensor_scalar, T.wv[:, :], T.pa[:, 3:5], -1.0, float(2 * 16 * NB), Op.mult, Op.add)
+
+    t_base = []
+    t_sc, t_hd = {}, {}
+    for chi in range(2):
+        col = ASW * chi
+        t_sc[chi] = run("V", [t_in, t_w, t_b[2 * chi + 1], t_b[2 * chi]], v.tensor_tensor_scan, T.pa[:, B * chi:B * chi + B], T.sums[:, col + 1:col + 1 + B],
+                        T.pb[:, B * chi:B * chi + B], T.init[:, chi:chi + 1], Op.add, Op.subtract)
+        t_hd[chi] = run("S", [t_sc[chi], t_lane], s.activation, T.hd[:, B * chi:B * chi + B], T.pa[:, B * chi:B * chi + B], Fn.Copy, scale=T.lf[:, 2:3])
+    for chi in range(2):
+        own = T.base[:, STR * chi + B * rank:STR * chi + B * rank + B]
+        t_base.append(run("V", [t_hd[chi]], v.tensor_tensor, own, T.pa[:, B * chi:B * chi + B], T.hd[:, B * chi:B * chi + B], Op.subtract))
+        send([t_base[chi]], own, "bin%d" % chi)
+    t = run("V", [t_w], v.tensor_scalar, T.wd[:, :], T.wv[:, :], T.lf[:, 2:3], None, Op.mult)
+    t_end = run("V", [t, t_ones], v.tensor_tensor, T.base[:, NB:W:STR], T.wv[:, :], T.wd[:, :], Op.subtract)
+
+    of = [T.of0, T.of1]
+    pend = [("bin0", arrived), ("bin1", arrived), t_end]
+    ps = [T.pa[:, 1024:1088], T.pa[:, 1536:1600]]
+    free = [t_base[1], t_hd[1]]
+    t_x = []
+    for st in range(8):
+        o, P = of[st % 2], ps[st % 2]
+        run("P", free + [t_eq, t_ch], pe.matmul, T.pa[:, 0:512], T.idm[:, :], T.nh[:, :], True, False)
+        run("P", [], pe.matmul, T.pa[:, 512:1024], T.idm[:, :], T.nh[:, :], True, False)
+        run("P", [], pe.matmul, P, T.idm[:, :], T.c8[:, :], True, False)
+        if st < 7:
+            run("P", [], pe.matmul, P, T.idm[:, :], T.ch2[:, st + 1, :], False, False)
+        for h in range(2):
+            for q in range(16):
+                run("P", [t_kl], pe.matmul, T.pa[:, 512 * h + q:512 * h + 512:16], T.xq[:, 128 * q:128 * q + 128],
+                    T.kl[:, st % 2, 32 * h:32 * h + 32], False, False)
+        t_kg, t_y, t_ym = [], [], []
+        for h in range(2):
+            t_kg.append(run("S", [t_of, dma_dup, ("kin", arrived)] if st == 0 else [t_of], s.activation, T.kg[:, 512 * h:512 * h + 512],
+                            T.keyw[:, 0:W].indirect(o[:, 32 * h:32 * h + 32]), Fn.Copy))
+            t_ym.append(run("V", [t_of, t_m[st]] + pend, v.tensor_tensor, T.ym[:, 512 * h:512 * h + 512],
+                            T.base[:, 0:W].indirect(o[:, 32 * h:32 * h + 32]), T.msk[:, 512 * st:512 * st + 512], Op.mult))
+        for h in range(2):
+            t_y.append(run("P", [t_kg[h]], pe.matmul, T.pa[:, 512 * h:512 * h + 512], T.neg[:, :], T.kg[:, 512 * h:512 * h + 512], False, True))
+        t_xa = run("S", [t_y[0]], s.activation, T.xs[:, 0:512], T.pa[:, 0:512], Fn.Sign)
+        t_xb = run("V", [t_y[1]], v.tensor_scalar, T.xs[:, 512:1024], T.pa[:, 512:1024], 0.0, 2.0, Op.is_gt, Op.mult)
+        for q in range(16):
+            run("P", [t_ym[1]], pe.matmul, P, T.eq[:, 128 * q:128 * q + 128], T.ym[:, q::16], False, False)
+        for q in range(16):
+            t_p = run("P", [t_xa, t_xb], pe.matmul, P, T.eq[:, 128 * q:128 * q + 128], T.xs[:, q::16], False, q == 15)
+        free = []
+        if st < 7:
+            t_of = run("V", [t_p], v.tensor_scalar, of[1 - st % 2][:, :], P, 0.0625, -0.46875, Op.mult, Op.add)
+            t = run("V", [], v.tensor_copy, T.xi[:, :], P)
+            t = run("V", [t], v.tensor_scalar, T.ri[:, :], T.xi[:, :], 15, None, Op.bitwise_and)
+            t_kl = run("V", [t], v.tensor_tensor, T.kl[:, 1 - st % 2, :], T.ri[:, :], T.c16[:, st + 1, :], Op.add)
+        else:
+            t = run("V", [t_p], v.tensor_copy, T.yo[:, :], P)
+            dma("Y", [t], "out", T.y[:, :], T.yo[:, :])
+
+    for sem in ["cV", "cS", "cP", "cG", "dup", "out", "snt"]:
+        need("G", [(sem, total[sem])])

@@ -1,11 +1,12 @@
 from concourse.bass import DstId, RemoteDMATransfer
-from concourse.mybir import AluOpType as Op, ActivationFunctionType as Fn
+from concourse.mybir import AluOpType as Op, ActivationFunctionType as Fn, AxisListType
 
 R, B = 4, 1024
 NB = R * B
 STR = 4224
 W = 2 * STR
 ASW = 1032
+HC = 384
 
 SCRATCH = {
     "raw": ("sbuf", [128, 64, 16], "int32"),
@@ -16,51 +17,42 @@ SCRATCH = {
     "feat": ("sbuf", [128, 16 * B], "bfloat16"),
     "sums": ("sbuf", [128, 2 * ASW], "bfloat16"),
     "hd": ("sbuf", [128, 2 * B], "bfloat16"),
-    "tot": ("sbuf", [128, R, 8], "float32"),
-    "t2": ("sbuf", [128, R, 2], "float32"),
-    "pre": ("sbuf", [128, R, 2], "float32"),
+    "tot": ("sbuf", [128, 2 * 4 * R], "float32"),
     "rr": ("sbuf", [128, 8], "float32"),
-    "q1": ("sbuf", [128, 2], "float32"),
-    "init": ("sbuf", [128, 2], "float32"),
+    "init": ("sbuf", [128, 8], "float32"),
     "wv": ("sbuf", [128, 2], "float32"),
     "wd": ("sbuf", [128, 2], "bfloat16"),
     "gi": ("sbuf", [128, 128], "bfloat16"),
-    "j1": ("sbuf", [128, 128], "bfloat16"),
     "j8": ("sbuf", [128, 128], "bfloat16"),
-    "d0": ("sbuf", [128, 128], "bfloat16"),
     "lp": ("sbuf", [128, 1], "int32"),
     "li": ("sbuf", [128, 4], "int32"),
     "lf": ("sbuf", [128, 4], "float32"),
     "ma": ("sbuf", [128, 128], "bfloat16"),
     "mb": ("sbuf", [128, 128], "bfloat16"),
     "bm": ("sbuf", [128, 128], "bfloat16"),
-    "f16": ("sbuf", [128, 128], "bfloat16"),
     "f8": ("sbuf", [128, 128], "bfloat16"),
     "lfm": ("sbuf", [128, 8 * 128], "bfloat16"),
     "xq": ("sbuf", [128, 16 * 128], "bfloat16"),
     "eq": ("sbuf", [128, 16 * 128], "bfloat16"),
     "idm": ("sbuf", [128, 128], "bfloat16"),
     "neg": ("sbuf", [128, 128], "bfloat16"),
-    "s1": ("sbuf", [128, 128], "float32"),
     "s2": ("sbuf", [128, 128], "float32"),
-    "s3": ("sbuf", [128, 128], "float32"),
     "s4": ("sbuf", [128, 128], "float32"),
     "smf": ("sbuf", [128, 128], "float32"),
     "swf": ("sbuf", [128, 128], "float32"),
     "smb": ("sbuf", [128, 128], "bfloat16"),
     "swb": ("sbuf", [128, 128], "bfloat16"),
-    "nh": ("sbuf", [128, 512], "bfloat16"),
     "c8": ("sbuf", [128, 64], "bfloat16"),
     "pat": ("sbuf", [128, 8, 32], "int32"),
     "pi": ("sbuf", [128, 8, 32], "int32"),
     "chi": ("sbuf", [128, 8, 32], "int32"),
     "cl": ("sbuf", [128, 8, 32], "bfloat16"),
     "ch2": ("sbuf", [128, 8, 64], "bfloat16"),
-    "c16": ("sbuf", [128, 8, 64], "bfloat16"),
+    "clx": ("sbuf", [128, 8 * 512], "bfloat16"),
     "msk": ("sbuf", [128, 8 * 512], "bfloat16"),
     "sti": ("sbuf", [128, 64], "int32"),
-    "xi": ("sbuf", [128, 64], "int32"),
-    "ri": ("sbuf", [128, 64], "int32"),
+    "sf": ("sbuf", [128, 2, 64], "float32"),
+    "oi": ("sbuf", [128, 64], "int32"),
     "kl": ("sbuf", [128, 2, 64], "bfloat16"),
     "of0": ("sbuf", [128, 64], "uint16"),
     "of1": ("sbuf", [128, 64], "uint16"),
@@ -71,12 +63,45 @@ SCRATCH = {
     "pa": ("psum", [128, 2048], "float32"),
     "pb": ("psum", [128, 2048], "float32"),
 }
-SEMAPHORES = ["cV", "cS", "cP", "cG", "lpat", "lst", "dup", "out", "kin", "tin", "bin0", "bin1", "snt"] + ["ld%d" % k for k in range(8)]
+SEMAPHORES = ["cV", "cS", "cP", "cG", "lpat", "lst", "out", "hk", "hb0", "hb1", "kin", "tin0", "tin1",
+              "bin0", "bin1", "snt"] + ["ld%d" % k for k in range(8)]
+
+
+def helper(rank_core, T, topo):
+    for c in topo.cores_of(rank_core):
+        if topo.die(c) != topo.die(rank_core) and all(topo.may_write(c, d) for d in T.cores if d != rank_core):
+            return c
+
+
+def route(core, to, topo):
+    ids, mask = [], None
+    for c in to:
+        rid, pid = topo.addr(c)[:2]
+        ids.append(DstId(rid=rid, pnc=pid))
+        mask = topo.mask(core, c) if mask is None else mask & topo.mask(core, c)
+    return ids, mask, bin(mask).count("1")
+
+
+def hand_on(g, core, rank, T, topo):
+    ids, mask, width = route(core, [c for c in T.cores if c != T.cores[rank]], topo)
+    came = route(T.cores[rank], [core], topo)[2]
+    sent = 0
+    for buf, at, n, here, there in [(T.keyw, 0, B, "hk", "kin"), (T.base, STR, HC, "hb1", "bin1"), (T.base, 0, HC, "hb0", "bin0")]:
+        piece = buf[:, at + B * rank:at + B * rank + n]
+        g.wait_ge(T.sem[here], came)
+        g.remote_dma_fused([RemoteDMATransfer(dst_ids=ids, dma_engine_mask=mask, remote_sem=T.sem[there],
+                                              srcs=[piece], dsts=[piece for _ in ids], alu_op=0)],
+                           local_sem=T.sem.snt)
+        sent += width
+    g.wait_ge(T.sem.snt, sent)
 
 
 def rank_program(g, core, T, topo):
     rank = T.rank_of(core)
     if rank is None:
+        for r, c in enumerate(T.cores):
+            if helper(c, T, topo) == core:
+                hand_on(g, core, r, T, topo)
         return
     queues = {"V": g.vector, "S": g.scalar, "P": g.tensor, "G": g, "Y": g.sync}
     total, seen = {}, {}
@@ -102,23 +127,18 @@ def rank_program(g, core, T, topo):
 
     v, s, pe = g.vector, g.scalar, g.tensor
     others = [c for c in T.cores if c != core]
-    mask = topo.mask(core, others[0])
-    for c in others[1:]:
-        mask &= topo.mask(core, c)
-    width = bin(mask).count("1")
-    ids = []
-    for c in others:
-        rid, pid = topo.addr(c)[:2]
-        ids.append(DstId(rid=rid, pnc=pid))
+    hand = helper(core, T, topo)
+    ids, mask, width = route(core, others, topo)
+    hid, hmask, hwidth = route(core, [hand], topo)
+    hw = route(hand, others, topo)[2]
+    k_in, t_in, b_in = hw * (R - 1), width * (R - 1), (hw + width) * (R - 1)
 
-    def send(deps, piece, sem):
+    def send(deps, piece, sem, to=ids, eng=mask, n=width):
         need("G", deps)
-        g.remote_dma_fused([RemoteDMATransfer(dst_ids=ids, dma_engine_mask=mask, remote_sem=T.sem[sem],
-                                              srcs=[piece], dsts=[piece for _ in ids], alu_op=0)],
+        g.remote_dma_fused([RemoteDMATransfer(dst_ids=to, dma_engine_mask=eng, remote_sem=T.sem[sem],
+                                              srcs=[piece], dsts=[piece for _ in to], alu_op=0)],
                            local_sem=T.sem.snt)
-        total["snt"] = total.get("snt", 0) + width
-
-    arrived = width * len(others)
+        total["snt"] = total.get("snt", 0) + n
 
     ld = []
     for k in range(8):
@@ -132,155 +152,176 @@ def rank_program(g, core, T, topo):
     g_lp = run("G", [], g.iota, T.lp[:, :], [[0, 1]], 0, 1)
     g_gi = run("G", [], g.iota, T.gi[:, :], [[-16, 8], [0, 16]], 0, 1, **fl)
     g_j8 = run("G", [], g.iota, T.j8[:, :], [[0, 16], [1, 8]], 1, 0, **fl)
-    g_j1 = run("G", [], g.iota, T.j1[:, :], [[0, 8], [1, 16]], 1, 0, **fl)
-    g_d0 = run("G", [], g.iota, T.d0[:, :], [[-1, 128]], 0, 1, **fl)
 
-    run("V", [], v.memset, T.feat[:, 0:B], 1.0)
+    t_ones = run("V", [], v.memset, T.feat[:, 0:B], 1.0)
     run("V", [], v.memset, T.sums[:, 0:1], 0.0)
     run("V", [], v.memset, T.sums[:, ASW:ASW + 1], 0.0)
-    run("V", [], v.memset, T.keyw[:, NB:STR], 1024.0)
-    run("V", [], v.memset, T.base[:, NB:STR], 0.0)
-    t_ones = run("V", [], v.memset, T.base[:, STR + NB:W], 0.0)
+    run("V", [], v.memset, T.tot[:, 4 * rank:4 * rank + 4], 0.0)
+    run("V", [], v.memset, T.tot[:, 4 * (R + rank):4 * (R + rank) + 4], 0.0)
+    t_rr = run("V", [], v.memset, T.rr[:, :], 0.0)
     run("V", [g_lp], v.tensor_scalar, T.li[:, 0:1], T.lp[:, :], 15, None, Op.bitwise_and)
     run("V", [], v.tensor_scalar, T.li[:, 1:2], T.lp[:, :], 7, None, Op.bitwise_and)
     t = run("V", [], v.tensor_scalar, T.li[:, 2:3], T.lp[:, :], 3, 1, Op.arith_shift_right, Op.bitwise_and)
     run("V", [g_gi], v.tensor_scalar, T.ma[:, :], T.gi[:, :], 0.0, None, Op.is_ge)
     t2 = run("V", [], v.tensor_scalar, T.mb[:, :], T.gi[:, :], 15.0, None, Op.is_le)
-    t_lane = run("V", [t], v.tensor_copy, T.lf[:, 0:3], T.li[:, 0:3])
+    run("V", [t], v.tensor_scalar, T.lf[:, 0:1], T.li[:, 0:1], 0.0625, None, Op.mult)
+    t_lane = run("V", [], v.tensor_copy, T.lf[:, 1:3], T.li[:, 1:3])
     t3 = run("V", [t2], v.tensor_tensor, T.bm[:, :], T.ma[:, :], T.mb[:, :], Op.mult)
-    t4 = run("V", [t3, g_j8], v.tensor_tensor, T.f8[:, :], T.bm[:, :], T.j8[:, :], Op.mult)
+    run("V", [g_j8], v.tensor_scalar, T.s2[:, :], T.j8[:, :], 8.0, None, Op.is_lt)
+    t_s24 = run("V", [], v.tensor_scalar, T.s4[:, :], T.j8[:, :], 8.0, None, Op.is_ge)
+    t4 = run("V", [t3], v.tensor_tensor, T.f8[:, :], T.bm[:, :], T.j8[:, :], Op.mult)
     for y in range(8):
-        t_lfm = run("V", [t4], v.tensor_scalar, T.lfm[:, 128 * y:128 * y + 128], T.f8[:, :], float(y + 1), None, Op.is_equal)
+        t_lfm = run("V", [t4], v.tensor_scalar, T.lfm[:, 128 * y:128 * y + 128], T.f8[:, :], float(y + 1), 2.0, Op.is_equal, Op.mult)
+    run("G", [t_s24], g.affine_select, T.smf[:, :], T.s2[:, :], [[-1, 128]], Op.is_equal, 0.0, -1, 1)
+    g_sh = run("G", [], g.affine_select, T.swf[:, :], T.s4[:, :], [[-1, 128]], Op.is_equal, 0.0, 7, 1)
+    g_id = run("G", [t_ones], g.affine_select, T.idm[:, :], T.feat[:, 0:128], [[-1, 128]], Op.is_equal, 0.0, 0, 1)
+    run("S", [t_ones], s.activation, T.c8[:, 0:32], T.feat[:, 0:32], Fn.Copy, scale=0.46875)
+    run("S", [], s.activation, T.c8[:, 32:64], T.feat[:, 0:32], Fn.Copy, scale=-0.03125)
+    run("S", [g_sh], s.activation, T.smb[:, :], T.smf[:, :], Fn.Copy)
+    t_sh = run("S", [], s.activation, T.swb[:, :], T.swf[:, :], Fn.Copy)
+    t_neg = run("S", [g_id], s.activation, T.neg[:, :], T.idm[:, :], Fn.Copy, scale=-1.0)
 
     for k in range(8):
         j, y = k // 2, k % 2
         t = run("V", [ld[k]], v.tensor_copy, T.half[:, :, 32 * j + 16 * y:32 * j + 16 * y + 16], T.raw[:, 8 * k:8 * k + 8, :])
     for i in range(8):
         t_let = run("V", [t], v.transpose, T.let[:, i::8], T.half[:, i, :])
-    t_key = run("V", [t_let, t_lane], v.tensor_scalar, T.keyw[:, B * rank:B * rank + B], T.let[:, :], 16.0, T.lf[:, 0:1], Op.mult, Op.add)
-    send([t_key], T.keyw[:, B * rank:B * rank + B], "kin")
-    dma_dup = dma("Y", [t_key, ("kin", arrived)], "dup", T.keyw[:, STR:W], T.keyw[:, 0:STR])
+    t_key = run("V", [t_let, t_lane], v.tensor_scalar, T.keyw[:, B * rank:B * rank + B], T.let[:, :], T.lf[:, 0:1], None, Op.add)
+    send([t_key], T.keyw[:, B * rank:B * rank + B], "hk", hid, hmask, hwidth)
+    run("G", [], g.affine_select, T.xq[:, 0:1024], T.feat[:, 0:1024], [[-1, 8], [-16, 8], [0, 16]], Op.is_equal, 0.0, 0, 1)
+    g_xq = run("G", [], g.affine_select, T.xq[:, 1024:2048], T.feat[:, 0:1024], [[-1, 8], [-16, 8], [0, 16]], Op.is_equal, 0.0, -8, 1)
 
-    t_f = [t_ones]
-    for c in range(1, 16):
-        t_f.append(run("V", [], v.tensor_scalar, T.feat[:, B * c:B * c + B], T.let[:, :], float(c), None, Op.is_ge))
-    t_a = {}
-    for c in range(16):
+    t_f = {0: t_ones}
+    for c in list(range(8, 16)) + list(range(1, 8)):
+        t_f[c] = run("V", [], v.tensor_scalar, T.feat[:, B * c:B * c + B], T.let[:, :], float(c), None, Op.is_ge)
+    t_b, t_s, t_ini, t_v = {}, {}, {}, {}
+
+    def count(chi):
+        for c in range(8 * chi, 8 * chi + 8):
+            for h in range(2):
+                at = B * chi + 512 * h
+                t = run("P", [t_f[c], t_lfm], pe.matmul, T.pa[:, at:at + 512], T.lfm[:, 128 * (c % 8):128 * (c % 8) + 128],
+                        T.feat[:, B * c + 512 * h:B * c + 512 * h + 512], c % 8 == 0, c % 8 == 7)
+        return t
+
+    def own(chi):
+        return 4 * (R * chi + rank)
+
+    def shifted(chi, deps):
         for h in range(2):
-            bank = 2 * (c // 8) + h
-            t_a[bank] = run("P", [t_f[c], t_lfm], pe.matmul, T.pa[:, 512 * bank:512 * bank + 512], T.lfm[:, 128 * (c % 8):128 * (c % 8) + 128],
-                            T.feat[:, B * c + 512 * h:B * c + 512 * h + 512], c % 8 == 0, c % 8 == 7)
-    t_s = {}
-    for bank in range(4):
-        at = ASW * (bank // 2) + 1 + 512 * (bank % 2)
-        t_s[bank] = run("S", [t_a[bank], t_ones], s.activation, T.sums[:, at:at + 512], T.pa[:, 512 * bank:512 * bank + 512],
-                        Fn.Copy, scale=2.0, accum_out=T.tot[:, rank, bank:bank + 1])
-    send([t_s[3]], T.tot[:, rank, 0:4], "tin")
+            out = T.pb[:, B * chi + 512 * h:B * chi + 512 * h + 512]
+            t_b[chi] = run("P", t_s[chi] + [t_sh] + deps, pe.matmul, out, T.smb[:, :],
+                           T.sums[:, ASW * chi + 512 * h:ASW * chi + 512 * h + 512], True, chi == 1)
+            if chi == 0:
+                t_b[chi] = run("P", [], pe.matmul, out, T.swb[:, :], T.sums[:, ASW + 512 * h:ASW + 512 * h + 512], False, True)
 
-    run("V", [g_d0], v.tensor_scalar, T.s1[:, :], T.d0[:, :], 1.0, None, Op.is_equal)
-    run("V", [], v.tensor_scalar, T.s2[:, :], T.j8[:, :], 8.0, None, Op.is_lt)
-    run("V", [], v.tensor_scalar, T.s3[:, :], T.d0[:, :], -7.0, None, Op.is_equal)
-    t = run("V", [], v.tensor_scalar, T.s4[:, :], T.j8[:, :], 8.0, None, Op.is_equal)
-    run("V", [t], v.tensor_tensor, T.smf[:, :], T.s1[:, :], T.s2[:, :], Op.mult)
-    run("V", [], v.tensor_tensor, T.swf[:, :], T.s3[:, :], T.s4[:, :], Op.mult)
-    run("V", [], v.tensor_tensor, T.smb[:, :], T.s1[:, :], T.s2[:, :], Op.mult)
-    t_sh = run("V", [], v.tensor_tensor, T.swb[:, :], T.s3[:, :], T.s4[:, :], Op.mult)
-    t_b = {}
-    for bank in range(4):
-        chi, h = bank // 2, bank % 2
-        out = T.pb[:, 512 * bank:512 * bank + 512]
-        t_b[bank] = run("P", [t_s[3], t_sh], pe.matmul, out, T.smb[:, :], T.sums[:, ASW * chi + 512 * h:ASW * chi + 512 * h + 512], True, chi == 1)
+    def begin(chi, bank, deps):
+        col, lo, mid, hi = 4 * chi, 4 * R * chi, own(chi), 4 * R * (chi + 1)
+        need("V", [("tin%d" % chi, t_in), t_rr] + t_s[chi])
+        if rank:
+            run("V", [], v.tensor_reduce, T.rr[:, col:col + 1], T.tot[:, lo:mid], AxisListType.X, Op.add)
+        t_t = run("V", [], v.tensor_reduce, T.rr[:, col + 1:col + 2], T.tot[:, lo:hi], AxisListType.X, Op.add)
+        t = run("V", [], v.tensor_reduce, T.init[:, col:col + 1], T.tot[:, mid:hi], AxisListType.X, Op.add, negate=True)
+        pt = T.pb[:, 512 * bank:512 * bank + 2]
+        t_pt = run("P", [t_t, t_sh, g_sh] + deps, pe.matmul, pt, T.smf[:, :], T.rr[:, col:col + 2], True, chi == 1)
         if chi == 0:
-            t_b[bank] = run("P", [], pe.matmul, out, T.swb[:, :], T.sums[:, ASW + 512 * h:ASW + 512 * h + 512], False, True)
+            t_pt = run("P", [], pe.matmul, pt, T.swf[:, :], T.rr[:, 4:6], False, True)
+        t = run("V", [t], v.tensor_scalar, T.init[:, col + 1:col + 2], T.init[:, col:col + 1], float(2 * (16 * NB - 16)), None, Op.add)
+        t_ini[chi] = run("V", [t, t_pt], v.tensor_tensor, T.init[:, col + 2:col + 3], T.init[:, col + 1:col + 2], pt[:, 0:1], Op.subtract)
+        t_v[chi] = run("V", [], v.tensor_scalar, T.wv[:, chi:chi + 1], pt[:, 1:2], -1.0, float(2 * 16 * NB), Op.mult, Op.add)
 
+    def table(chi):
+        t_sc, start, t_hd = t_ini[chi], T.init[:, 4 * chi + 2:4 * chi + 3], []
+        for h in range(2):
+            at, sc = B * chi + 512 * h, ASW * chi + 1 + 512 * h
+            t_sc = run("V", [t_sc, t_b[chi]] + t_s[chi], v.tensor_tensor_scan, T.pa[:, at:at + 512], T.sums[:, sc:sc + 512],
+                       T.pb[:, at:at + 512], start, Op.add, Op.subtract)
+            if h == 0:
+                start = T.init[:, 4 * chi + 3:4 * chi + 4]
+                t_sc = run("V", [t_sc], v.tensor_copy, start, T.pa[:, at + 511:at + 512])
+            t_hd.append(run("S", [t_sc, t_lane], s.activation, T.hd[:, at:at + 512], T.pa[:, at:at + 512], Fn.Copy, scale=T.lf[:, 2:3]))
+        for h, (a, e) in enumerate([(0, HC), (HC, B)]):
+            at, to = B * chi, STR * chi + B * rank
+            t = run("V", [t_hd[h]], v.tensor_tensor, T.base[:, to + a:to + e], T.pa[:, at + a:at + e], T.hd[:, at + a:at + e], Op.subtract)
+            if h == 0:
+                send([t], T.base[:, to + a:to + e], "hb%d" % chi, hid, hmask, hwidth)
+            else:
+                send([t], T.base[:, to + a:to + e], "bin%d" % chi)
+        return t
+
+    def total_of(chi):
+        return T.tot[:, own(chi):own(chi) + 1]
+
+    t = count(1)
+    t_s[1] = [run("S", [t, t_ones, t_rr], s.activation, T.sums[:, ASW + 1:ASW + 1 + B], T.pa[:, B:2 * B], Fn.Copy, accum_out=total_of(1))]
+    send(t_s[1], T.tot[:, own(1):own(1) + 4], "tin1")
+    t = count(0)
+    t_s0 = run("S", [t], s.activation, T.sums[:, 1:513], T.pa[:, 0:512], Fn.Copy, accum_out=total_of(0))
+    t_s1 = run("V", [t], v.tensor_reduce, T.tot[:, own(0) + 1:own(0) + 2], T.pa[:, 512:1024], AxisListType.X, Op.add)
+    send([t_s0, t_s1], T.tot[:, own(0):own(0) + 4], "tin0")
+    t_s[0] = [t_s0, run("V", [], v.tensor_copy, T.sums[:, 513:1025], T.pa[:, 512:1024])]
+    shifted(1, [])
+    begin(1, 0, [])
+    table(1)
+    shifted(0, [t_v[1]])
+    begin(0, 2, [t_v[1], t_b[1]])
+    t_tab = table(0)
+
+    run("V", [], v.memset, T.keyw[:, NB:STR], 1024.0)
+    run("V", [], v.memset, T.base[:, NB:STR], 0.0)
+    t_pad = run("V", [], v.memset, T.base[:, STR + NB:W], 0.0)
+    t = run("V", [t_v[0]], v.tensor_scalar, T.wd[:, :], T.wv[:, :], T.lf[:, 2:3], None, Op.mult)
     run("V", [lpat], v.tensor_scalar, T.pi[:, :, :], T.pat[:, :, :], 7, None, Op.bitwise_and)
-    t = run("V", [], v.tensor_scalar, T.chi[:, :, :], T.pat[:, :, :], 3, None, Op.arith_shift_right)
-    for q in range(16):
-        t_xq = run("V", [], v.tensor_scalar, T.xq[:, 128 * q:128 * q + 128], T.gi[:, :], float(q), None, Op.is_equal)
-    t_cl = run("V", [t], v.tensor_copy, T.cl[:, :, :], T.pi[:, :, :])
-    t_m = {}
+    t_ci = run("V", [], v.tensor_scalar, T.chi[:, :, :], T.pat[:, :, :], 3, None, Op.arith_shift_right)
+    t_end = run("V", [t, t_pad], v.tensor_tensor, T.base[:, NB:W:STR], T.wv[:, :], T.wd[:, :], Op.subtract)
+    t_cl = run("V", [t_ci], v.tensor_copy, T.cl[:, :, :], T.pi[:, :, :])
+    for h in range(2):
+        t_ch = run("V", [], v.tensor_scalar, T.ch2[:, :, 32 * h:32 * h + 32], T.chi[:, :, :], float(STR), None, Op.mult)
+    t_c, t_m = {}, {}
     for st in range(8):
         bank = st % 4
-        deps = [t_cl, t_xq, t_s[3]] + ([t_m[st - 4]] if st >= 4 else [])
+        deps = [t_cl, g_xq, t_tab] + ([t_c[st - 4]] if st >= 4 else [])
         for q in range(16):
             lo = 512 * bank + q
-            t_ex = run("P", deps, pe.matmul, T.pa[:, lo:512 * bank + 512:16], T.xq[:, 128 * q:128 * q + 128], T.cl[:, st, :], True, True)
-        if st == 0:
-            t = run("V", [g_j1], v.tensor_tensor, T.f16[:, :], T.bm[:, :], T.j1[:, :], Op.mult)
+            t = run("P", deps, pe.matmul, T.pa[:, lo:512 * bank + 512:16], T.xq[:, 128 * q:128 * q + 128], T.cl[:, st, :], True, True)
+        t_c[st] = run("S", [t], s.activation, T.clx[:, 512 * st:512 * st + 512], T.pa[:, 512 * bank:512 * bank + 512], Fn.Copy)
+        if st == 3:
             for q in range(16):
-                t_eq = run("V", [t], v.tensor_scalar, T.eq[:, 128 * q:128 * q + 128], T.f16[:, :], float(q + 1), 0.5, Op.is_equal, Op.mult)
-            run("V", [], v.tensor_scalar, T.idm[:, :], T.d0[:, :], 0.0, None, Op.is_equal)
-            run("V", [], v.tensor_scalar, T.neg[:, :], T.d0[:, :], 0.0, -1.0, Op.is_equal, Op.mult)
-            run("V", [], v.memset, T.nh[:, :], -0.5)
-            run("V", [], v.memset, T.c8[:, 0:32], 8.0)
-            run("V", [], v.memset, T.c8[:, 32:64], 0.0)
-            run("V", [], v.memset, T.rr[:, :], 0.0)
-            for h in range(2):
-                run("V", [], v.tensor_scalar, T.ch2[:, :, 32 * h:32 * h + 32], T.chi[:, :, :], float(STR * 16), None, Op.mult)
-                t_ch = run("V", [], v.tensor_scalar, T.c16[:, :, 32 * h:32 * h + 32], T.pat[:, :, :], 16.0, None, Op.mult)
-            t = run("V", [t_ch, lst], v.tensor_tensor, T.xi[:, :], T.sti[:, :], T.ch2[:, 0, :], Op.add)
-            t_of = run("V", [t], v.tensor_scalar, T.of0[:, :], T.xi[:, :], 0.0625, -0.46875, Op.mult, Op.add)
-            t = run("V", [], v.tensor_scalar, T.ri[:, :], T.xi[:, :], 15, None, Op.bitwise_and)
-            t_kl = run("V", [t], v.tensor_tensor, T.kl[:, 0, :], T.ri[:, :], T.c16[:, 0, :], Op.add)
-        t_m[st] = run("V", [t_ex, t_lane], v.tensor_scalar, T.msk[:, 512 * st:512 * st + 512], T.pa[:, 512 * bank:512 * bank + 512],
+                t = run("P", [g_id], pe.matmul, T.pb[:, 128 * q:128 * q + 128], T.xq[:, 128 * q:128 * q + 128], T.idm[:, :], True, True)
+            for i in range(4):
+                t_eq = run("S", [t], s.activation, T.eq[:, 512 * i:512 * i + 512], T.pb[:, 512 * i:512 * i + 512], Fn.Copy, scale=0.03125)
+    t = run("V", [lst], v.tensor_scalar, T.sf[:, 0, :], T.sti[:, :], 0.0625, -0.03125, Op.mult, Op.add)
+    t = run("V", [t, t_ch], v.tensor_tensor, T.sf[:, 1, :], T.sf[:, 0, :], T.ch2[:, 0, :], Op.add)
+    t_of = run("V", [t], v.tensor_scalar, T.of0[:, :], T.sf[:, 1, :], -0.4375, None, Op.add)
+    t = run("V", [], v.tensor_scalar, T.oi[:, :], T.sf[:, 1, :], -0.4375, None, Op.add)
+    t_kl = run("V", [t], v.tensor_tensor, T.kl[:, 0, :], T.sf[:, 1, :], T.oi[:, :], Op.subtract)
+    for st in range(8):
+        t_m[st] = run("V", [t_c[st], t_lane], v.tensor_scalar, T.msk[:, 512 * st:512 * st + 512], T.clx[:, 512 * st:512 * st + 512],
                       T.lf[:, 1:2], None, Op.is_equal)
-
-    need("V", [("tin", arrived), t_s[3]])
-    t = run("V", [], v.tensor_tensor, T.t2[:, :, :], T.tot[:, :, 0:4:2], T.tot[:, :, 1:4:2], Op.add)
-    acc, t_acc, pre = T.t2[:, 0, :], t, None
-    for r in range(1, R):
-        if r == rank:
-            pre = acc
-        dst = T.rr[:, 3:5] if r == R - 1 else T.pre[:, r, :]
-        t_acc = run("V", [t_acc], v.tensor_tensor, dst, acc, T.t2[:, r, :], Op.add)
-        acc = dst
-    t = t_acc
-    if pre is not None:
-        t = run("V", [t_acc], v.tensor_copy, T.rr[:, 0:2], pre)
-    run("P", [t, t_m[7], t_sh], pe.matmul, T.pa[:, 0:5], T.smf[:, :], T.rr[:, 0:5], True, False)
-    t_pt = run("P", [], pe.matmul, T.pa[:, 0:5], T.swf[:, :], T.rr[:, 1:6], False, True)
-    t = run("V", [t], v.tensor_tensor, T.q1[:, :], T.rr[:, 0:2], T.rr[:, 3:5], Op.subtract)
-    t = run("V", [t], v.tensor_scalar, T.q1[:, :], T.q1[:, :], float(2 * (16 * NB - 16)), None, Op.add)
-    t_in = run("V", [t, t_pt], v.tensor_tensor, T.init[:, :], T.q1[:, :], T.pa[:, 0:2], Op.subtract)
-    t_w = run("V", [], v.tensor_scalar, T.wv[:, :], T.pa[:, 3:5], -1.0, float(2 * 16 * NB), Op.mult, Op.add)
-
-    t_base = []
-    t_sc, t_hd = {}, {}
-    for chi in range(2):
-        col = ASW * chi
-        t_sc[chi] = run("V", [t_in, t_w, t_b[2 * chi + 1], t_b[2 * chi]], v.tensor_tensor_scan, T.pa[:, B * chi:B * chi + B], T.sums[:, col + 1:col + 1 + B],
-                        T.pb[:, B * chi:B * chi + B], T.init[:, chi:chi + 1], Op.add, Op.subtract)
-        t_hd[chi] = run("S", [t_sc[chi], t_lane], s.activation, T.hd[:, B * chi:B * chi + B], T.pa[:, B * chi:B * chi + B], Fn.Copy, scale=T.lf[:, 2:3])
-    for chi in range(2):
-        own = T.base[:, STR * chi + B * rank:STR * chi + B * rank + B]
-        t_base.append(run("V", [t_hd[chi]], v.tensor_tensor, own, T.pa[:, B * chi:B * chi + B], T.hd[:, B * chi:B * chi + B], Op.subtract))
-        send([t_base[chi]], own, "bin%d" % chi)
-    t = run("V", [t_w], v.tensor_scalar, T.wd[:, :], T.wv[:, :], T.lf[:, 2:3], None, Op.mult)
-    t_end = run("V", [t, t_ones], v.tensor_tensor, T.base[:, NB:W:STR], T.wv[:, :], T.wd[:, :], Op.subtract)
+        if st == 3:
+            t_dup = run("V", [("kin", k_in), t_pad], v.tensor_scalar, T.keyw[:, STR:W], T.keyw[:, 0:STR], -8.0, None, Op.add)
 
     of = [T.of0, T.of1]
-    pend = [("bin0", arrived), ("bin1", arrived), t_end]
+    pend = [("bin1", b_in), ("bin0", b_in), t_end]
     ps = [T.pa[:, 1024:1088], T.pa[:, 1536:1600]]
-    free = [t_base[1], t_hd[1]]
-    t_x = []
+    free = [t_c[7], t_eq, t_ch, t_neg]
     for st in range(8):
         o, P = of[st % 2], ps[st % 2]
-        run("P", free + [t_eq, t_ch], pe.matmul, T.pa[:, 0:512], T.idm[:, :], T.nh[:, :], True, False)
-        run("P", [], pe.matmul, T.pa[:, 512:1024], T.idm[:, :], T.nh[:, :], True, False)
+        for h in range(2):
+            run("P", free, pe.matmul, T.pa[:, 512 * h:512 * h + 512], T.idm[:, :], T.clx[:, 512 * st:512 * st + 512], True, False)
         run("P", [], pe.matmul, P, T.idm[:, :], T.c8[:, :], True, False)
         if st < 7:
             run("P", [], pe.matmul, P, T.idm[:, :], T.ch2[:, st + 1, :], False, False)
-        for h in range(2):
-            for q in range(16):
-                run("P", [t_kl], pe.matmul, T.pa[:, 512 * h + q:512 * h + 512:16], T.xq[:, 128 * q:128 * q + 128],
-                    T.kl[:, st % 2, 32 * h:32 * h + 32], False, False)
         t_kg, t_y, t_ym = [], [], []
         for h in range(2):
-            t_kg.append(run("S", [t_of, dma_dup, ("kin", arrived)] if st == 0 else [t_of], s.activation, T.kg[:, 512 * h:512 * h + 512],
+            t_kg.append(run("S", [t_of, t_dup], s.activation, T.kg[:, 512 * h:512 * h + 512],
                             T.keyw[:, 0:W].indirect(o[:, 32 * h:32 * h + 32]), Fn.Copy))
             t_ym.append(run("V", [t_of, t_m[st]] + pend, v.tensor_tensor, T.ym[:, 512 * h:512 * h + 512],
                             T.base[:, 0:W].indirect(o[:, 32 * h:32 * h + 32]), T.msk[:, 512 * st:512 * st + 512], Op.mult))
         for h in range(2):
+            for q in range(16):
+                run("P", [t_kl], pe.matmul, T.pa[:, 512 * h + q:512 * h + 512:16], T.xq[:, 128 * q:128 * q + 128],
+                    T.kl[:, st % 2, 32 * h:32 * h + 32], False, False)
             t_y.append(run("P", [t_kg[h]], pe.matmul, T.pa[:, 512 * h:512 * h + 512], T.neg[:, :], T.kg[:, 512 * h:512 * h + 512], False, True))
         t_xa = run("S", [t_y[0]], s.activation, T.xs[:, 0:512], T.pa[:, 0:512], Fn.Sign)
         t_xb = run("V", [t_y[1]], v.tensor_scalar, T.xs[:, 512:1024], T.pa[:, 512:1024], 0.0, 2.0, Op.is_gt, Op.mult)
@@ -290,13 +331,12 @@ def rank_program(g, core, T, topo):
             t_p = run("P", [t_xa, t_xb], pe.matmul, P, T.eq[:, 128 * q:128 * q + 128], T.xs[:, q::16], False, q == 15)
         free = []
         if st < 7:
-            t_of = run("V", [t_p], v.tensor_scalar, of[1 - st % 2][:, :], P, 0.0625, -0.46875, Op.mult, Op.add)
-            t = run("V", [], v.tensor_copy, T.xi[:, :], P)
-            t = run("V", [t], v.tensor_scalar, T.ri[:, :], T.xi[:, :], 15, None, Op.bitwise_and)
-            t_kl = run("V", [t], v.tensor_tensor, T.kl[:, 1 - st % 2, :], T.ri[:, :], T.c16[:, st + 1, :], Op.add)
+            t_of = run("V", [t_p], v.tensor_scalar, of[1 - st % 2][:, :], P, -0.4375, None, Op.add)
+            t = run("V", [], v.tensor_scalar, T.oi[:, :], P, -0.4375, None, Op.add)
+            t_kl = run("V", [t], v.tensor_tensor, T.kl[:, 1 - st % 2, :], P, T.oi[:, :], Op.subtract)
         else:
-            t = run("V", [t_p], v.tensor_copy, T.yo[:, :], P)
+            t = run("V", [t_p], v.tensor_scalar, T.yo[:, :], P, 16.0, 0.5, Op.mult, Op.add)
             dma("Y", [t], "out", T.y[:, :], T.yo[:, :])
 
-    for sem in ["cV", "cS", "cP", "cG", "dup", "out", "snt"]:
+    for sem in ["cV", "cS", "cP", "cG", "out", "snt"]:
         need("G", [(sem, total[sem])])

from concourse.bass import DstId, RemoteDMATransfer
from concourse.mybir import AluOpType as Op, ActivationFunctionType as Fn, AxisListType

R, B = 4, 1024
NB = R * B
STR = 4224
W = 2 * STR
ASW = 1032
HC = 384

SCRATCH = {
    "raw": ("sbuf", [128, 64, 16], "int32"),
    "half": ("sbuf", [128, 8, 128], "bfloat16"),
    "let": ("sbuf", [128, B], "bfloat16"),
    "keyw": ("sbuf", [128, W], "bfloat16"),
    "base": ("sbuf", [128, W], "bfloat16"),
    "feat": ("sbuf", [128, 16 * B], "bfloat16"),
    "sums": ("sbuf", [128, 2 * ASW], "bfloat16"),
    "hd": ("sbuf", [128, 2 * B], "bfloat16"),
    "tot": ("sbuf", [128, 2 * 4 * R], "float32"),
    "rr": ("sbuf", [128, 8], "float32"),
    "init": ("sbuf", [128, 8], "float32"),
    "wv": ("sbuf", [128, 2], "float32"),
    "wd": ("sbuf", [128, 2], "bfloat16"),
    "gi": ("sbuf", [128, 128], "bfloat16"),
    "j8": ("sbuf", [128, 128], "bfloat16"),
    "lp": ("sbuf", [128, 1], "int32"),
    "li": ("sbuf", [128, 4], "int32"),
    "lf": ("sbuf", [128, 4], "float32"),
    "ma": ("sbuf", [128, 128], "bfloat16"),
    "mb": ("sbuf", [128, 128], "bfloat16"),
    "bm": ("sbuf", [128, 128], "bfloat16"),
    "f8": ("sbuf", [128, 128], "bfloat16"),
    "lfm": ("sbuf", [128, 8 * 128], "bfloat16"),
    "xq": ("sbuf", [128, 16 * 128], "bfloat16"),
    "eq": ("sbuf", [128, 16 * 128], "bfloat16"),
    "idm": ("sbuf", [128, 128], "bfloat16"),
    "neg": ("sbuf", [128, 128], "bfloat16"),
    "s2": ("sbuf", [128, 128], "float32"),
    "s4": ("sbuf", [128, 128], "float32"),
    "smf": ("sbuf", [128, 128], "float32"),
    "swf": ("sbuf", [128, 128], "float32"),
    "smb": ("sbuf", [128, 128], "bfloat16"),
    "swb": ("sbuf", [128, 128], "bfloat16"),
    "c8": ("sbuf", [128, 64], "bfloat16"),
    "pat": ("sbuf", [128, 8, 32], "int32"),
    "pi": ("sbuf", [128, 8, 32], "int32"),
    "chi": ("sbuf", [128, 8, 32], "int32"),
    "cl": ("sbuf", [128, 8, 32], "bfloat16"),
    "ch2": ("sbuf", [128, 8, 64], "bfloat16"),
    "clx": ("sbuf", [128, 8 * 512], "bfloat16"),
    "msk": ("sbuf", [128, 8 * 512], "bfloat16"),
    "sti": ("sbuf", [128, 64], "int32"),
    "sf": ("sbuf", [128, 2, 64], "float32"),
    "oi": ("sbuf", [128, 64], "int32"),
    "kl": ("sbuf", [128, 2, 64], "bfloat16"),
    "of0": ("sbuf", [128, 64], "uint16"),
    "of1": ("sbuf", [128, 64], "uint16"),
    "kg": ("sbuf", [128, 1024], "bfloat16"),
    "ym": ("sbuf", [128, 1024], "bfloat16"),
    "xs": ("sbuf", [128, 1024], "bfloat16"),
    "yo": ("sbuf", [128, 64], "float32"),
    "pa": ("psum", [128, 2048], "float32"),
    "pb": ("psum", [128, 2048], "float32"),
}
SEMAPHORES = ["cV", "cS", "cP", "cG", "lpat", "lst", "out", "hk", "hb0", "hb1", "kin", "tin0", "tin1",
              "bin0", "bin1", "snt"] + ["ld%d" % k for k in range(8)]


def helper(rank_core, T, topo):
    for c in topo.cores_of(rank_core):
        if topo.die(c) != topo.die(rank_core) and all(topo.may_write(c, d) for d in T.cores if d != rank_core):
            return c


def route(core, to, topo):
    ids, mask = [], None
    for c in to:
        rid, pid = topo.addr(c)[:2]
        ids.append(DstId(rid=rid, pnc=pid))
        mask = topo.mask(core, c) if mask is None else mask & topo.mask(core, c)
    return ids, mask, bin(mask).count("1")


def hand_on(g, core, rank, T, topo):
    ids, mask, width = route(core, [c for c in T.cores if c != T.cores[rank]], topo)
    came = route(T.cores[rank], [core], topo)[2]
    sent = 0
    for buf, at, n, here, there in [(T.keyw, 0, B, "hk", "kin"), (T.base, STR, HC, "hb1", "bin1"), (T.base, 0, HC, "hb0", "bin0")]:
        piece = buf[:, at + B * rank:at + B * rank + n]
        g.wait_ge(T.sem[here], came)
        g.remote_dma_fused([RemoteDMATransfer(dst_ids=ids, dma_engine_mask=mask, remote_sem=T.sem[there],
                                              srcs=[piece], dsts=[piece for _ in ids], alu_op=0)],
                           local_sem=T.sem.snt)
        sent += width
    g.wait_ge(T.sem.snt, sent)


def rank_program(g, core, T, topo):
    rank = T.rank_of(core)
    if rank is None:
        for r, c in enumerate(T.cores):
            if helper(c, T, topo) == core:
                hand_on(g, core, r, T, topo)
        return
    queues = {"V": g.vector, "S": g.scalar, "P": g.tensor, "G": g, "Y": g.sync}
    total, seen = {}, {}

    def need(q, deps):
        for sem, val in deps:
            if seen.get((q, sem), 0) < val:
                queues[q].wait_ge(T.sem[sem], val)
                seen[(q, sem)] = val

    def run(q, deps, f, *a, **kw):
        need(q, deps)
        sem = "c" + q
        f(*a, **kw).then_inc(T.sem[sem], 1)
        total[sem] = total.get(sem, 0) + 1
        return (sem, total[sem])

    def dma(q, deps, sem, out, in_):
        need(q, deps)
        queues[q].dma_start(out, in_).then_inc(T.sem[sem], 16)
        total[sem] = total.get(sem, 0) + 16
        return (sem, total[sem])

    v, s, pe = g.vector, g.scalar, g.tensor
    others = [c for c in T.cores if c != core]
    hand = helper(core, T, topo)
    ids, mask, width = route(core, others, topo)
    hid, hmask, hwidth = route(core, [hand], topo)
    hw = route(hand, others, topo)[2]
    k_in, t_in, b_in = hw * (R - 1), width * (R - 1), (hw + width) * (R - 1)

    def send(deps, piece, sem, to=ids, eng=mask, n=width):
        need("G", deps)
        g.remote_dma_fused([RemoteDMATransfer(dst_ids=to, dma_engine_mask=eng, remote_sem=T.sem[sem],
                                              srcs=[piece], dsts=[piece for _ in to], alu_op=0)],
                           local_sem=T.sem.snt)
        total["snt"] = total.get("snt", 0) + n

    ld = []
    for k in range(8):
        j, y = k // 2, k % 2
        ld.append(dma("Y" if k % 2 == 0 else "S", [], "ld%d" % k, T.raw[:, 8 * k:8 * k + 8, :],
                      T.bwt[y::2, 4096 * j:4096 * j + 4096]))
    lpat = dma("Y", [], "lpat", T.pat[:, :, :], T.pats[:, :])
    lst = dma("Y", [], "lst", T.sti[:, :], T.starts[:, :])

    fl = dict(allow_small_or_imprecise_dtypes=True)
    g_lp = run("G", [], g.iota, T.lp[:, :], [[0, 1]], 0, 1)
    g_gi = run("G", [], g.iota, T.gi[:, :], [[-16, 8], [0, 16]], 0, 1, **fl)
    g_j8 = run("G", [], g.iota, T.j8[:, :], [[0, 16], [1, 8]], 1, 0, **fl)

    t_ones = run("V", [], v.memset, T.feat[:, 0:B], 1.0)
    run("V", [], v.memset, T.sums[:, 0:1], 0.0)
    run("V", [], v.memset, T.sums[:, ASW:ASW + 1], 0.0)
    run("V", [], v.memset, T.tot[:, 4 * rank:4 * rank + 4], 0.0)
    run("V", [], v.memset, T.tot[:, 4 * (R + rank):4 * (R + rank) + 4], 0.0)
    t_rr = run("V", [], v.memset, T.rr[:, :], 0.0)
    run("V", [g_lp], v.tensor_scalar, T.li[:, 0:1], T.lp[:, :], 15, None, Op.bitwise_and)
    run("V", [], v.tensor_scalar, T.li[:, 1:2], T.lp[:, :], 7, None, Op.bitwise_and)
    t = run("V", [], v.tensor_scalar, T.li[:, 2:3], T.lp[:, :], 3, 1, Op.arith_shift_right, Op.bitwise_and)
    run("V", [g_gi], v.tensor_scalar, T.ma[:, :], T.gi[:, :], 0.0, None, Op.is_ge)
    t2 = run("V", [], v.tensor_scalar, T.mb[:, :], T.gi[:, :], 15.0, None, Op.is_le)
    run("V", [t], v.tensor_scalar, T.lf[:, 0:1], T.li[:, 0:1], 0.0625, None, Op.mult)
    t_lane = run("V", [], v.tensor_copy, T.lf[:, 1:3], T.li[:, 1:3])
    t3 = run("V", [t2], v.tensor_tensor, T.bm[:, :], T.ma[:, :], T.mb[:, :], Op.mult)
    run("V", [g_j8], v.tensor_scalar, T.s2[:, :], T.j8[:, :], 8.0, None, Op.is_lt)
    t_s24 = run("V", [], v.tensor_scalar, T.s4[:, :], T.j8[:, :], 8.0, None, Op.is_ge)
    t4 = run("V", [t3], v.tensor_tensor, T.f8[:, :], T.bm[:, :], T.j8[:, :], Op.mult)
    for y in range(8):
        t_lfm = run("V", [t4], v.tensor_scalar, T.lfm[:, 128 * y:128 * y + 128], T.f8[:, :], float(y + 1), 2.0, Op.is_equal, Op.mult)
    run("G", [t_s24], g.affine_select, T.smf[:, :], T.s2[:, :], [[-1, 128]], Op.is_equal, 0.0, -1, 1)
    g_sh = run("G", [], g.affine_select, T.swf[:, :], T.s4[:, :], [[-1, 128]], Op.is_equal, 0.0, 7, 1)
    g_id = run("G", [t_ones], g.affine_select, T.idm[:, :], T.feat[:, 0:128], [[-1, 128]], Op.is_equal, 0.0, 0, 1)
    run("S", [t_ones], s.activation, T.c8[:, 0:32], T.feat[:, 0:32], Fn.Copy, scale=0.46875)
    run("S", [], s.activation, T.c8[:, 32:64], T.feat[:, 0:32], Fn.Copy, scale=-0.03125)
    run("S", [g_sh], s.activation, T.smb[:, :], T.smf[:, :], Fn.Copy)
    t_sh = run("S", [], s.activation, T.swb[:, :], T.swf[:, :], Fn.Copy)
    t_neg = run("S", [g_id], s.activation, T.neg[:, :], T.idm[:, :], Fn.Copy, scale=-1.0)

    for k in range(8):
        j, y = k // 2, k % 2
        t = run("V", [ld[k]], v.tensor_copy, T.half[:, :, 32 * j + 16 * y:32 * j + 16 * y + 16], T.raw[:, 8 * k:8 * k + 8, :])
    for i in range(8):
        t_let = run("V", [t], v.transpose, T.let[:, i::8], T.half[:, i, :])
    t_key = run("V", [t_let, t_lane], v.tensor_scalar, T.keyw[:, B * rank:B * rank + B], T.let[:, :], T.lf[:, 0:1], None, Op.add)
    send([t_key], T.keyw[:, B * rank:B * rank + B], "hk", hid, hmask, hwidth)
    run("G", [], g.affine_select, T.xq[:, 0:1024], T.feat[:, 0:1024], [[-1, 8], [-16, 8], [0, 16]], Op.is_equal, 0.0, 0, 1)
    g_xq = run("G", [], g.affine_select, T.xq[:, 1024:2048], T.feat[:, 0:1024], [[-1, 8], [-16, 8], [0, 16]], Op.is_equal, 0.0, -8, 1)

    t_f = {0: t_ones}
    for c in list(range(8, 16)) + list(range(1, 8)):
        t_f[c] = run("V", [], v.tensor_scalar, T.feat[:, B * c:B * c + B], T.let[:, :], float(c), None, Op.is_ge)
    t_b, t_s, t_ini, t_v = {}, {}, {}, {}

    def count(chi):
        for c in range(8 * chi, 8 * chi + 8):
            for h in range(2):
                at = B * chi + 512 * h
                t = run("P", [t_f[c], t_lfm], pe.matmul, T.pa[:, at:at + 512], T.lfm[:, 128 * (c % 8):128 * (c % 8) + 128],
                        T.feat[:, B * c + 512 * h:B * c + 512 * h + 512], c % 8 == 0, c % 8 == 7)
        return t

    def own(chi):
        return 4 * (R * chi + rank)

    def shifted(chi, deps):
        for h in range(2):
            out = T.pb[:, B * chi + 512 * h:B * chi + 512 * h + 512]
            t_b[chi] = run("P", t_s[chi] + [t_sh] + deps, pe.matmul, out, T.smb[:, :],
                           T.sums[:, ASW * chi + 512 * h:ASW * chi + 512 * h + 512], True, chi == 1)
            if chi == 0:
                t_b[chi] = run("P", [], pe.matmul, out, T.swb[:, :], T.sums[:, ASW + 512 * h:ASW + 512 * h + 512], False, True)

    def begin(chi, bank, deps):
        col, lo, mid, hi = 4 * chi, 4 * R * chi, own(chi), 4 * R * (chi + 1)
        need("V", [("tin%d" % chi, t_in), t_rr] + t_s[chi])
        if rank:
            run("V", [], v.tensor_reduce, T.rr[:, col:col + 1], T.tot[:, lo:mid], AxisListType.X, Op.add)
        t_t = run("V", [], v.tensor_reduce, T.rr[:, col + 1:col + 2], T.tot[:, lo:hi], AxisListType.X, Op.add)
        t = run("V", [], v.tensor_reduce, T.init[:, col:col + 1], T.tot[:, mid:hi], AxisListType.X, Op.add, negate=True)
        pt = T.pb[:, 512 * bank:512 * bank + 2]
        t_pt = run("P", [t_t, t_sh, g_sh] + deps, pe.matmul, pt, T.smf[:, :], T.rr[:, col:col + 2], True, chi == 1)
        if chi == 0:
            t_pt = run("P", [], pe.matmul, pt, T.swf[:, :], T.rr[:, 4:6], False, True)
        t = run("V", [t], v.tensor_scalar, T.init[:, col + 1:col + 2], T.init[:, col:col + 1], float(2 * (16 * NB - 16)), None, Op.add)
        t_ini[chi] = run("V", [t, t_pt], v.tensor_tensor, T.init[:, col + 2:col + 3], T.init[:, col + 1:col + 2], pt[:, 0:1], Op.subtract)
        t_v[chi] = run("V", [], v.tensor_scalar, T.wv[:, chi:chi + 1], pt[:, 1:2], -1.0, float(2 * 16 * NB), Op.mult, Op.add)

    def table(chi):
        t_sc, start, t_hd = t_ini[chi], T.init[:, 4 * chi + 2:4 * chi + 3], []
        for h in range(2):
            at, sc = B * chi + 512 * h, ASW * chi + 1 + 512 * h
            t_sc = run("V", [t_sc, t_b[chi]] + t_s[chi], v.tensor_tensor_scan, T.pa[:, at:at + 512], T.sums[:, sc:sc + 512],
                       T.pb[:, at:at + 512], start, Op.add, Op.subtract)
            if h == 0:
                start = T.init[:, 4 * chi + 3:4 * chi + 4]
                t_sc = run("V", [t_sc], v.tensor_copy, start, T.pa[:, at + 511:at + 512])
            t_hd.append(run("S", [t_sc, t_lane], s.activation, T.hd[:, at:at + 512], T.pa[:, at:at + 512], Fn.Copy, scale=T.lf[:, 2:3]))
        for h, (a, e) in enumerate([(0, HC), (HC, B)]):
            at, to = B * chi, STR * chi + B * rank
            t = run("V", [t_hd[h]], v.tensor_tensor, T.base[:, to + a:to + e], T.pa[:, at + a:at + e], T.hd[:, at + a:at + e], Op.subtract)
            if h == 0:
                send([t], T.base[:, to + a:to + e], "hb%d" % chi, hid, hmask, hwidth)
            else:
                send([t], T.base[:, to + a:to + e], "bin%d" % chi)
        return t

    def total_of(chi):
        return T.tot[:, own(chi):own(chi) + 1]

    t = count(1)
    t_s[1] = [run("S", [t, t_ones, t_rr], s.activation, T.sums[:, ASW + 1:ASW + 1 + B], T.pa[:, B:2 * B], Fn.Copy, accum_out=total_of(1))]
    send(t_s[1], T.tot[:, own(1):own(1) + 4], "tin1")
    t = count(0)
    t_s0 = run("S", [t], s.activation, T.sums[:, 1:513], T.pa[:, 0:512], Fn.Copy, accum_out=total_of(0))
    t_s1 = run("V", [t], v.tensor_reduce, T.tot[:, own(0) + 1:own(0) + 2], T.pa[:, 512:1024], AxisListType.X, Op.add)
    send([t_s0, t_s1], T.tot[:, own(0):own(0) + 4], "tin0")
    t_s[0] = [t_s0, run("V", [], v.tensor_copy, T.sums[:, 513:1025], T.pa[:, 512:1024])]
    shifted(1, [])
    begin(1, 0, [])
    table(1)
    shifted(0, [t_v[1]])
    begin(0, 2, [t_v[1], t_b[1]])
    t_tab = table(0)

    run("V", [], v.memset, T.keyw[:, NB:STR], 1024.0)
    run("V", [], v.memset, T.base[:, NB:STR], 0.0)
    t_pad = run("V", [], v.memset, T.base[:, STR + NB:W], 0.0)
    t = run("V", [t_v[0]], v.tensor_scalar, T.wd[:, :], T.wv[:, :], T.lf[:, 2:3], None, Op.mult)
    run("V", [lpat], v.tensor_scalar, T.pi[:, :, :], T.pat[:, :, :], 7, None, Op.bitwise_and)
    t_ci = run("V", [], v.tensor_scalar, T.chi[:, :, :], T.pat[:, :, :], 3, None, Op.arith_shift_right)
    t_end = run("V", [t, t_pad], v.tensor_tensor, T.base[:, NB:W:STR], T.wv[:, :], T.wd[:, :], Op.subtract)
    t_cl = run("V", [t_ci], v.tensor_copy, T.cl[:, :, :], T.pi[:, :, :])
    for h in range(2):
        t_ch = run("V", [], v.tensor_scalar, T.ch2[:, :, 32 * h:32 * h + 32], T.chi[:, :, :], float(STR), None, Op.mult)
    t_c, t_m = {}, {}
    for st in range(8):
        bank = st % 4
        deps = [t_cl, g_xq, t_tab] + ([t_c[st - 4]] if st >= 4 else [])
        for q in range(16):
            lo = 512 * bank + q
            t = run("P", deps, pe.matmul, T.pa[:, lo:512 * bank + 512:16], T.xq[:, 128 * q:128 * q + 128], T.cl[:, st, :], True, True)
        t_c[st] = run("S", [t], s.activation, T.clx[:, 512 * st:512 * st + 512], T.pa[:, 512 * bank:512 * bank + 512], Fn.Copy)
        if st == 3:
            for q in range(16):
                t = run("P", [g_id], pe.matmul, T.pb[:, 128 * q:128 * q + 128], T.xq[:, 128 * q:128 * q + 128], T.idm[:, :], True, True)
            for i in range(4):
                t_eq = run("S", [t], s.activation, T.eq[:, 512 * i:512 * i + 512], T.pb[:, 512 * i:512 * i + 512], Fn.Copy, scale=0.03125)
    t = run("V", [lst], v.tensor_scalar, T.sf[:, 0, :], T.sti[:, :], 0.0625, -0.03125, Op.mult, Op.add)
    t = run("V", [t, t_ch], v.tensor_tensor, T.sf[:, 1, :], T.sf[:, 0, :], T.ch2[:, 0, :], Op.add)
    t_of = run("V", [t], v.tensor_scalar, T.of0[:, :], T.sf[:, 1, :], -0.4375, None, Op.add)
    t = run("V", [], v.tensor_scalar, T.oi[:, :], T.sf[:, 1, :], -0.4375, None, Op.add)
    t_kl = run("V", [t], v.tensor_tensor, T.kl[:, 0, :], T.sf[:, 1, :], T.oi[:, :], Op.subtract)
    for st in range(8):
        t_m[st] = run("V", [t_c[st], t_lane], v.tensor_scalar, T.msk[:, 512 * st:512 * st + 512], T.clx[:, 512 * st:512 * st + 512],
                      T.lf[:, 1:2], None, Op.is_equal)
        if st == 3:
            t_dup = run("V", [("kin", k_in), t_pad], v.tensor_scalar, T.keyw[:, STR:W], T.keyw[:, 0:STR], -8.0, None, Op.add)

    of = [T.of0, T.of1]
    pend = [("bin1", b_in), ("bin0", b_in), t_end]
    ps = [T.pa[:, 1024:1088], T.pa[:, 1536:1600]]
    free = [t_c[7], t_eq, t_ch, t_neg]
    for st in range(8):
        o, P = of[st % 2], ps[st % 2]
        for h in range(2):
            run("P", free, pe.matmul, T.pa[:, 512 * h:512 * h + 512], T.idm[:, :], T.clx[:, 512 * st:512 * st + 512], True, False)
        run("P", [], pe.matmul, P, T.idm[:, :], T.c8[:, :], True, False)
        if st < 7:
            run("P", [], pe.matmul, P, T.idm[:, :], T.ch2[:, st + 1, :], False, False)
        t_kg, t_y, t_ym = [], [], []
        for h in range(2):
            t_kg.append(run("S", [t_of, t_dup], s.activation, T.kg[:, 512 * h:512 * h + 512],
                            T.keyw[:, 0:W].indirect(o[:, 32 * h:32 * h + 32]), Fn.Copy))
            t_ym.append(run("V", [t_of, t_m[st]] + pend, v.tensor_tensor, T.ym[:, 512 * h:512 * h + 512],
                            T.base[:, 0:W].indirect(o[:, 32 * h:32 * h + 32]), T.msk[:, 512 * st:512 * st + 512], Op.mult))
        for h in range(2):
            for q in range(16):
                run("P", [t_kl], pe.matmul, T.pa[:, 512 * h + q:512 * h + 512:16], T.xq[:, 128 * q:128 * q + 128],
                    T.kl[:, st % 2, 32 * h:32 * h + 32], False, False)
            t_y.append(run("P", [t_kg[h]], pe.matmul, T.pa[:, 512 * h:512 * h + 512], T.neg[:, :], T.kg[:, 512 * h:512 * h + 512], False, True))
        t_xa = run("S", [t_y[0]], s.activation, T.xs[:, 0:512], T.pa[:, 0:512], Fn.Sign)
        t_xb = run("V", [t_y[1]], v.tensor_scalar, T.xs[:, 512:1024], T.pa[:, 512:1024], 0.0, 2.0, Op.is_gt, Op.mult)
        for q in range(16):
            run("P", [t_ym[1]], pe.matmul, P, T.eq[:, 128 * q:128 * q + 128], T.ym[:, q::16], False, False)
        for q in range(16):
            t_p = run("P", [t_xa, t_xb], pe.matmul, P, T.eq[:, 128 * q:128 * q + 128], T.xs[:, q::16], False, q == 15)
        free = []
        if st < 7:
            t_of = run("V", [t_p], v.tensor_scalar, of[1 - st % 2][:, :], P, -0.4375, None, Op.add)
            t = run("V", [], v.tensor_scalar, T.oi[:, :], P, -0.4375, None, Op.add)
            t_kl = run("V", [t], v.tensor_tensor, T.kl[:, 1 - st % 2, :], P, T.oi[:, :], Op.subtract)
        else:
            t = run("V", [t_p], v.tensor_scalar, T.yo[:, :], P, 16.0, 0.5, Op.mult, Op.add)
            dma("Y", [t], "out", T.y[:, :], T.yo[:, :])

    for sem in ["cV", "cS", "cP", "cG", "out", "snt"]:
        need("G", [(sem, total[sem])])
